import numpy as np
import ml_dtypes


def mxq(x, axis, fmt="e4m3"):
    dtype, down = {"e4m3": (ml_dtypes.float8_e4m3fn, 7), "e5m2": (ml_dtypes.float8_e5m2, 14)}[fmt]
    v = np.moveaxis(np.asarray(x, np.float32).astype(ml_dtypes.bfloat16).astype(np.float64), axis, -1)
    blocks = v.reshape(v.shape[:-1] + (-1, 32))
    amax = np.abs(blocks).max(-1, keepdims=True)
    byte = np.maximum(np.where(amax > 0, np.frexp(amax)[1] - 1 + 127, 0) - down, 1)
    scale = np.exp2(byte - 127.0)
    codes = (blocks / scale).astype(np.float32).astype(dtype).astype(np.float64)
    return np.moveaxis((codes * scale).reshape(v.shape), -1, axis)


WIDE = False


def mx_kscale(k):
    if not WIDE:
        return np.ones(k)
    levels = np.array([10, -10, 5, -5, 0])
    if k % 512:
        return np.exp2(np.random.permutation(np.resize(levels, k // 32))).repeat(32)
    a = np.empty((k // 512, 16))
    for p in range(k // 512):
        a[p, :8] = np.random.permutation(np.resize(levels, 8))
        for g in range(8):
            far = levels[np.abs(levels - a[p, g]) >= 10]
            a[p, g + 8] = far[np.random.randint(len(far))]
    return np.exp2(a.ravel()).repeat(32)


BF16 = ml_dtypes.bfloat16


def bf(x):
    return np.asarray(x, np.float32).astype(BF16)


def f64(x):
    return np.asarray(x).astype(np.float64)


E2M1 = np.array([0.0, 0.5, 1.0, 1.5, 2.0, 3.0, 4.0, 6.0, -0.0, -0.5, -1.0, -1.5, -2.0, -3.0, -4.0, -6.0])


def pack_weight(w, fmt):
    k, n = w.shape
    w = f64(bf(w)).reshape(k // 32, 32, n)
    amax = np.abs(w).max(1)
    if fmt == "e4m3":
        byte = np.frexp(amax)[1] - 1 + 127 - 7
    else:
        mant, ex = np.frexp(amax / 6.0)
        byte = np.where(mant > 0.5, ex, ex - 1) + 127
    byte = np.clip(np.where(amax > 0, byte, 1), 1, 254)
    scaled = (w * np.exp2(127.0 - byte)[:, None, :]).reshape(k, n).astype(np.float32)
    by_word = np.ascontiguousarray(scaled.reshape(k // 512, 128, 4, n).transpose(0, 1, 3, 2))
    if fmt == "e4m3":
        words = by_word.astype(ml_dtypes.float8_e4m3fn).view(np.uint8)
    else:
        c = by_word.astype(ml_dtypes.float4_e2m1fn).view(np.uint8) & 0xF
        words = c[..., 0::2] | (c[..., 1::2] << 4)
    return np.ascontiguousarray(words), np.ascontiguousarray(byte.astype(np.uint8).reshape(k // 512, 16, n))


def unpack_weight(words, scales, fmt):
    g, p, n, _ = words.shape
    if fmt == "e4m3":
        vals = np.ascontiguousarray(words).view(ml_dtypes.float8_e4m3fn).astype(np.float64)
    else:
        nib = np.empty((g, p, n, 4), np.uint8)
        nib[..., 0::2] = words & 0xF
        nib[..., 1::2] = words >> 4
        vals = E2M1[nib]
    vals = vals * np.repeat(np.exp2(scales.astype(np.float64) - 127.0), 8, axis=1)[..., None]
    return vals.transpose(0, 1, 3, 2).reshape(g * 512, n)
def pack4(w):
    words, scales = pack_weight(w, "e2m1")
    return words.reshape(words.shape[0], 128, -1), scales


def unpack4(words, scales):
    return unpack_weight(words.reshape(words.shape[0], 128, -1, 2), scales, "e2m1")


def planes(Y):
    n, m = Y.shape
    b = f64(bf(Y)).reshape(n // 32, 32, m)
    amax = np.abs(b).max(1)
    byte = np.clip(np.where(amax > 0, np.frexp(amax)[1] - 1 + 127 - 7, 1), 1, 254)
    codes = (b * np.exp2(127.0 - byte)[:, None, :]).reshape(n, m).astype(np.float32).astype(ml_dtypes.float8_e4m3fn).view(np.uint8)
    words = codes.reshape(n // 512, 128, 4, m).transpose(0, 1, 3, 2)
    return np.ascontiguousarray(words), np.ascontiguousarray(byte.astype(np.uint8).reshape(n // 512, 16, m))


M, D, R, N = 1536, 2048, 512, 2048


def setup_inputs():
    s = mx_kscale(D)
    t = mx_kscale(R)
    x = np.random.randn(D, M) * s[:, None]
    down = np.random.randn(D, R) / np.sqrt(D) / s[:, None]
    x_words, x_scales = pack_weight(x, "e4m3")
    down_words, down_scales = pack4(down)
    rank_scale = (1 + 0.2 * np.random.randn(R)) * t
    up = np.random.randn(R, N) / np.sqrt(R) / t[:, None]
    spread = np.exp(0.8 * np.random.randn(N))
    out_scale = spread * (1 + 0.1 * np.random.randn(N))
    base = np.random.randn(M, N) * spread
    return {"x_words": x_words, "x_scales": x_scales,
            "down_words": down_words, "down_scales": down_scales,
            "rank_scale": bf(rank_scale), "up": bf(up),
            "out_scale": bf(out_scale), "base": bf(base)}


def reference(x_words, x_scales, down_words, down_scales, rank_scale, up, out_scale, base):
    xt = unpack_weight(x_words, x_scales, "e4m3")
    down = unpack4(down_words, down_scales)
    h = (xt.T @ down) * f64(rank_scale)
    u = mxq(h, 1, "e4m3") @ mxq(f64(up), 0, "e4m3")
    y = f64(base) + u * f64(out_scale)
    Y = y.T
    words, scales = planes(Y)
    return y, words, scales

from contextlib import ExitStack

import concourse.mybir as mybir
from concourse.masks import make_identity

M, D, R, N = 1536, 2048, 512, 2048
FLOPS = 2 * M * D * R + 2 * M * R * N

F32 = mybir.dt.float32
BF16 = mybir.dt.bfloat16
U32 = mybir.dt.uint32
I32 = mybir.dt.int32
U8 = mybir.dt.uint8
FP8X4 = mybir.dt.float8_e4m3fn_x4
FP4X4 = mybir.dt.float4_e2m1fn_x4
ALU = mybir.AluOpType
ACT = mybir.ActivationFunctionType

P = 128
G = 4
CHUNKS = [512, 512, 512]
X_PIECES = [256, 256, 256, 256, 512]
CASTS = ["ppvv", "ppvv", "aaav"]
WCOPY = ["aa", "aa", "aa"]
LAST_GROUPS = [(0, 2), (2, 4)]
HEAD = "S0u S1u I002v I024a M0 M1 U0 S2w T0t C0 T1t C1 O0 Q0 Q1 M2 S3w M3 S4h I102a T2t T3t C2 C3 Q2 Q3 M4 I124v"
UPS = {0: "U1 I204v U2", 1: "I304v U3"}
PIN = {mybir.EngineType.PE, mybir.EngineType.SP}
UP_PIECES = [(0, 1), (1, 2), (2, 4)]
SINGLE = 4
FINE = 10
HEAD_TILES = 5
LOADS = "ds dw x0 s0 u01 x1 x2 u12 s x3 u24 b0 b1 b2 b3 x4 b4 b5 b6 b7 b8 b9 b10 b11"
RS_ROW = 16
FIRST = 768
YBUFS = 3


def tile_scaled_adapter_to_head_h2_kernel(
    tc, x_words, x_scales, down_words, down_scales, rank_scale, up, out_scale, base, out_0, out_1, out_2
):
    nc = tc.nc
    starts = [sum(CHUNKS[:c]) for c in range(len(CHUNKS))]
    units = [(c, g) for c in range(len(CHUNKS)) for g in range(G)]
    chunk_of_tile = [c for c, w in enumerate(CHUNKS) for j in range(w // P)]

    with ExitStack() as ctx:
        keep = ctx.enter_context(tc.tile_pool(name="keep", bufs=1))
        work = ctx.enter_context(tc.tile_pool(name="work", bufs=2))
        psum = ctx.enter_context(tc.psum_pool(name="psum", bufs=1))
        ctx.enter_context(tc.manual_schedule(engines=PIN))

        ident = keep.tile([P, P], F32)
        vec_rows = keep.tile([P, P], BF16)
        vec_f32 = keep.tile([P, P], F32)
        cols = keep.tile([P, 16], F32)
        rs_col = keep.tile([P, 4], BF16)
        rs_f32 = keep.tile([P, 4], F32)
        rs_all = keep.tile([P, R], F32)
        dn_codes = keep.tile([P, G, 2 * R], U8, align_bytes=64)
        dn_scales = keep.tile([P, G, R], U8, align_bytes=64)
        x_starts = [sum(X_PIECES[:i]) for i in range(len(X_PIECES))]
        piece_of_tile = [i for i, w in enumerate(X_PIECES) for j in range(w // P)]
        x_codes = [keep.tile([P, G, w], U32, name=f"x_codes{i}", align_bytes=64) for i, w in enumerate(X_PIECES)]
        xs_first = keep.tile([P, G, FIRST], U8, align_bytes=64)
        xs_rest = keep.tile([P, G, M - FIRST], U8, align_bytes=64)
        base_sb = [keep.tile([P, N], BF16, name=f"base{n}") for n in range(M // P)]
        up_raw = {lo: keep.tile([P, 4, 512 * (hi - lo)], BF16, name=f"up_raw{lo}") for lo, hi in UP_PIECES}
        up_piece = {g: lo for lo, hi in UP_PIECES for g in range(lo, hi)}
        up_codes = [keep.tile([P, 512], U32, name=f"up_codes{g}", align_bytes=64) for g in range(G)]
        up_scales = [keep.tile([P, 512], U8, name=f"up_scales{g}", align_bytes=64) for g in range(G)]
        h_codes = [keep.tile([P, w], U32, name=f"h_codes{c}", align_bytes=64) for c, w in enumerate(CHUNKS)]
        h_scales = [keep.tile([P, w], U8, name=f"h_scales{c}", align_bytes=64) for c, w in enumerate(CHUNKS)]
        y_scales = [keep.tile([P, w], U8, name=f"y_scales{c}", align_bytes=64) for c, w in enumerate(CHUNKS)]

        def load_scale_rows(plane, rows):
            for q in range(4):
                nc.sync.dma_start(
                    out=plane[32 * q : 32 * q + 4, :, :].bitcast(I32),
                    in_=rows[:, 4 * q : 4 * q + 4, :].rearrange("g r n -> r g n").bitcast(I32),
                )

        def load_x(c):
            words = x_words.rearrange("g p n t -> p g (n t)")[:, :, 4 * x_starts[c] : 4 * (x_starts[c] + X_PIECES[c])]
            nc.sync.dma_start(out=x_codes[c][:].bitcast(I32), in_=words.bitcast(I32))

        def load_up(lo, hi):
            nc.sync.dma_start(
                out=up_raw[lo][:],
                in_=up[:, 512 * lo : 512 * hi].rearrange("(p j) n -> p j n", j=4),
            )

        def load_base(n):
            nc.sync.dma_start(out=base_sb[n][:], in_=base[P * n : P * (n + 1), :])

        nc.sync.dma_start(out=rs_col[:], in_=rank_scale.rearrange("(p t) -> p t", t=4))
        nc.vector.memset(dn_scales[:].bitcast(U32), 0)
        nc.vector.memset(xs_first[:].bitcast(U32), 0)
        nc.vector.memset(vec_rows[:].bitcast(U32), 0)
        nc.vector.memset(xs_rest[:].bitcast(U32), 0)
        make_identity(nc, ident[:])
        nc.gpsimd.dma_start(out=vec_rows[0:16, :], in_=out_scale.rearrange("(c p) -> c p", p=P))

        for item in LOADS.split():
            if item == "dw":
                nc.sync.dma_start(out=dn_codes[:].bitcast(I32), in_=down_words.rearrange("g p n -> p g n").bitcast(I32))
            elif item == "ds":
                load_scale_rows(dn_scales, down_scales)
            elif item == "s0":
                load_scale_rows(xs_first, x_scales[:, :, 0:FIRST])
            elif item == "s":
                load_scale_rows(xs_rest, x_scales[:, :, FIRST:M])
            elif item[0] == "u":
                load_up(int(item[1]), int(item[2]))
            elif item[0] == "x":
                load_x(int(item[1]))
            else:
                load_base(int(item[1:]))

        nc.vector.tensor_copy(out=rs_f32[:], in_=rs_col[:])
        rs_t = psum.tile([P, 4, P], F32, tag="bank", bufs=8)
        for t in range(4):
            nc.tensor.transpose(rs_t[:, t, :], rs_f32[:, t : t + 1].to_broadcast([P, P]), ident[:])
        nc.scalar.copy(
            out=rs_all[:].rearrange("m (u p e) -> m u p e", u=2, e=2),
            in_=rs_t[:].rearrange("m (u e) p -> m u p e", u=2),
        )

        def out_scale_columns():
            nc.vector.tensor_copy(out=vec_f32[:], in_=vec_rows[:])
            vec_t = psum.tile([P, P], F32, tag="bank", bufs=8)
            nc.tensor.transpose(vec_t[:], vec_f32[:], ident[:])
            nc.scalar.copy(out=cols[:], in_=vec_t[:, 0:16])

        live = {}

        def up_interleave(g, lo, hi, eng):
            if lo == 0:
                live["up_in", g] = work.tile([P, 512, 4], BF16, name="up_in", align_bytes=64, bufs=2)
            src = up_raw[up_piece[g]][:, :, 512 * (g - up_piece[g]) + lo : 512 * (g - up_piece[g]) + hi].rearrange("p j n -> p n j")
            dst = live["up_in", g][:, lo:hi, :]
            if eng == "a":
                nc.scalar.copy(out=dst, in_=src)
            elif eng == "p":
                nc.gpsimd.tensor_scalar(out=dst, in0=src, scalar1=1.0, scalar2=0.0, op0=ALU.mult, op1=ALU.add)
            else:
                nc.vector.tensor_copy(out=dst, in_=src)

        def up_quantize(g):
            nc.vector.quantize_mx(
                out=up_codes[g][:].bitcast(FP8X4),
                scales=up_scales[g][:],
                in_=live.pop(("up_in", g))[:].rearrange("p n j -> p (n j)"),
            )

        def down_matmul(n, tag, bufs):
            c = piece_of_tile[n]
            local = slice(P * n - x_starts[c], P * (n + 1) - x_starts[c])
            if P * n < FIRST:
                xs = xs_first[:, :, P * n : P * (n + 1)]
            else:
                xs = xs_rest[:, :, P * n - FIRST : P * (n + 1) - FIRST]
            h_ps = psum.tile([P, R], F32, tag="bank", bufs=8)
            live["h_ps", n] = h_ps
            for g in range(G):
                nc.tensor.matmul_mx(
                    out=h_ps[:],
                    lhsT=x_codes[c][:, g, local].bitcast(FP8X4),
                    lhsT_scale=xs[:, g, :],
                    rhs=dn_codes[:, g, :].bitcast(FP4X4),
                    rhs_scale=dn_scales[:, g, :],
                    start=(g == 0),
                    stop=(g == G - 1),
                )

        def h_scale(n):
            h_bf = work.tile([P, 2, P, 2], BF16, bufs=3)
            live["h_bf", n] = h_bf
            nc.vector.tensor_tensor(
                out=h_bf[:],
                in0=live.pop(("h_ps", n))[:].rearrange("m (p u e) -> m u p e", u=2, e=2),
                in1=rs_all[:].rearrange("m (u p e) -> m u p e", u=2, e=2),
                op=ALU.mult,
            )

        def h_transpose(n, tag, bufs):
            ht_ps = psum.tile([P, 2, P], F32, tag="bank", bufs=8)
            live["ht_ps", n] = ht_ps
            words = live.pop(("h_bf", n))[:].rearrange("m u p e -> m (u p e)").bitcast(F32)
            for u in range(2):
                nc.tensor.transpose(ht_ps[:, u, :], words[:, P * u : P * (u + 1)], ident[:])

        def h_copy(n):
            h_in = work.tile([P, 4 * P], BF16, align_bytes=64)
            live["h_in", n] = h_in
            nc.scalar.copy(
                out=h_in[:].bitcast(F32).rearrange("p (m u) -> p m u", u=2),
                in_=live.pop(("ht_ps", n))[:].rearrange("p u m -> p m u"),
            )

        def h_quantize(n):
            c = chunk_of_tile[n]
            local = slice(P * n - starts[c], P * (n + 1) - starts[c])
            nc.vector.quantize_mx(
                out=h_codes[c][:, local].bitcast(FP8X4), scales=h_scales[c][:, local], in_=live.pop(("h_in", n))[:]
            )

        def up_matmul(k, t, tag, bufs):
            c, g = units[k]
            u_ps = psum.tile([P, CHUNKS[c]], F32, tag="bank", bufs=8)
            live["u_ps", k, t] = u_ps
            feats = slice(P * t, P * (t + 1))
            nc.tensor.matmul_mx(
                out=u_ps[:],
                lhsT=up_codes[g][:, feats].bitcast(FP8X4),
                lhsT_scale=up_scales[g][:, feats],
                rhs=h_codes[c][:].bitcast(FP8X4),
                rhs_scale=h_scales[c][:],
                start=True,
                stop=True,
            )

        def u_scale(k, t, eng):
            c, g = units[k]
            if t == 0:
                live["v", k] = work.tile([P, 4, CHUNKS[c]], F32, name="v_sb")
            scale = cols[:, 4 * g + t : 4 * g + t + 1]
            src = live.pop(("u_ps", k, t))[:]
            if eng == "a":
                nc.scalar.activation(out=live["v", k][:, t, :], in_=src, func=ACT.Copy, scale=scale)
            else:
                nc.vector.tensor_scalar(out=live["v", k][:, t, :], in0=src, scalar1=scale, scalar2=None, op0=ALU.mult)

        def v_transpose(k, j):
            vt_ps = psum.tile([P, 4, P], F32, tag="bank", bufs=8)
            live["vt_ps", k, j] = vt_ps
            for t in range(4):
                nc.tensor.transpose(vt_ps[:, t, :], live["v", k][:, t, P * j : P * (j + 1)], ident[:])

        def add_base(k, j):
            c, g = units[k]
            if j == 0 and (g % 2 == 0 or k >= SINGLE):
                live["y", k] = work.tile([P, CHUNKS[c] // P, 1024], F32, name="y_sb", bufs=YBUFS)
                live["y", k + 1] = live["y", k]
            nc.vector.tensor_tensor(
                out=live["y", k][:, j, 512 * (g % 2) : 512 * (g % 2 + 1)],
                in0=live.pop(("vt_ps", k, j))[:].rearrange("m t p -> m (t p)"),
                in1=base_sb[starts[c] // P + j][:, 512 * g : 512 * (g + 1)],
                op=ALU.add,
            )

        def y_store(k, j0, j1, groups):
            c, g = units[k]
            rows = out_0[starts[c] + P * j0 : starts[c] + P * j1, 512 * (g + 1 - groups) : 512 * (g + 1)]
            nc.sync.dma_start(
                out=rows.rearrange("(j m) f -> m j f", m=P),
                in_=live["y", k][:, j0:j1, 512 * (g % 2 + 1 - groups) : 512 * (g % 2 + 1)],
            )

        def y_round(k, j, eng):
            y_bf = work.tile([P, 2, P, 2], BF16, bufs=8)
            live["y_bf", k, j] = y_bf
            g = units[k][1]
            src = live["y", k][:, j, 512 * (g % 2) : 512 * (g % 2 + 1)].rearrange("m (p u e) -> m u p e", u=2, e=2)
            if eng == "p":
                nc.gpsimd.tensor_scalar(out=y_bf[:], in0=src, scalar1=1.0, scalar2=0.0, op0=ALU.mult, op1=ALU.add)
            elif eng == "a":
                nc.scalar.copy(out=y_bf[:], in_=src)
            else:
                nc.vector.tensor_copy(out=y_bf[:], in_=src)

        def y_transpose(k, j0, j1):
            yt_ps = psum.tile([P, 2, (j1 - j0) * P], F32, tag="bank", bufs=8)
            live["yt_ps", k, j0] = yt_ps
            for j in range(j0, j1):
                words = live.pop(("y_bf", k, j))[:].rearrange("m u p e -> m (u p e)").bitcast(F32)
                for u in range(2):
                    nc.tensor.transpose(
                        yt_ps[:, u, P * (j - j0) : P * (j - j0 + 1)], words[:, P * u : P * (u + 1)], ident[:]
                    )

        def y_copy(k, j0, j1, eng):
            c, g = units[k]
            if j0 == 0:
                live["y_in", k] = work.tile([P, 4 * CHUNKS[c]], BF16, name="y_in", align_bytes=64)
            dst = live["y_in", k][:, 512 * j0 : 512 * j1]
            (nc.scalar.copy if eng == "a" else nc.vector.tensor_copy)(
                out=dst.bitcast(F32).rearrange("p (m u) -> p m u", u=2),
                in_=live.pop(("yt_ps", k, j0))[:].rearrange("p u m -> p m u"),
            )

        def y_quantize(k, j0, j1):
            c, g = units[k]
            y_codes = work.tile([P, P * (j1 - j0)], U32, bufs=4, align_bytes=64)
            nc.vector.quantize_mx(
                out=y_codes[:].bitcast(FP8X4),
                scales=y_scales[c][4 * g : P, P * j0 : P * j1],
                in_=live["y_in", k][:, 512 * j0 : 512 * j1],
            )
            words = out_1[g].rearrange("p m t -> p (m t)")[:, 4 * (starts[c] + P * j0) : 4 * (starts[c] + P * j1)]
            nc.sync.dma_start(out=words.bitcast(I32), in_=y_codes[:].bitcast(I32))

        def scale_store(c):
            for q in range(4):
                nc.sync.dma_start(
                    out=out_2[:, 4 * q : 4 * q + 4, starts[c] : starts[c] + CHUNKS[c]].bitcast(I32),
                    in_=y_scales[c][32 * q : 32 * q + 16, :].bitcast(I32),
                )

        banks = {"u": 2, "h": 1, "w": 2, "t": 3}
        for item in HEAD.split():
            op, n = item[0], int(item[1], 16)
            if op == "S":
                down_matmul(n, item[2], banks[item[2]])
            elif op == "M":
                h_scale(n)
            elif op == "T":
                h_transpose(n, item[2], banks[item[2]])
            elif op == "C":
                h_copy(n)
            elif op == "Q":
                h_quantize(n)
            elif op == "I":
                up_interleave(n, 128 * int(item[2]), 128 * int(item[3]), item[4])
            elif op == "U":
                up_quantize(n)
            elif op == "O":
                out_scale_columns()

        last = len(units) - 1
        for k in range(last + 2):
            has_u = k <= last
            n = HEAD_TILES + k
            side = n < M // P
            casts = CASTS[0] if side else CASTS[1] if has_u else CASTS[2]
            wcopy = WCOPY[0] if side else WCOPY[1] if has_u else WCOPY[2]
            if has_u:
                up_matmul(k, 0, "u", 2)
                up_matmul(k, 1, "u", 2)
                u_scale(k, 0, "a")
                u_scale(k, 1, "a")
            if side:
                down_matmul(n, "h", 1)
            if has_u:
                up_matmul(k, 2, "u", 2)
                up_matmul(k, 3, "u", 2)
                u_scale(k, 2, "a")
                u_scale(k, 3, "a")
            if side:
                h_scale(n)
            for item in UPS.get(k, "").split():
                if item[0] == "I":
                    up_interleave(int(item[1]), 128 * int(item[2]), 128 * int(item[3]), item[4])
                else:
                    up_quantize(int(item[1]))
            if k == 0:
                h_transpose(n - 1, "h", 1)
                h_copy(n - 1)
                h_quantize(n - 1)
            for j in range(4):
                if k >= 1:
                    v_transpose(k - 1, j)
                    add_base(k - 1, j)
                    if casts[j] != "v":
                        y_round(k - 1, j, casts[j])
                    if j >= 1 and casts[j - 1] == "v":
                        y_round(k - 1, j - 1, "v")
                    if k - 1 >= FINE:
                        y_store(k - 1, j, j + 1, 1)
                if j == 1 and side:
                    h_transpose(n, "h", 1)
                    h_copy(n)
                if not has_u and j % 2 == 1:
                    y_transpose(k - 2, j - 1, j + 1)
                    y_copy(k - 2, j - 1, j + 1, wcopy[j // 2])
            if k >= 2 and has_u:
                for i in range(2):
                    y_transpose(k - 2, 2 * i, 2 * i + 2)
                    y_copy(k - 2, 2 * i, 2 * i + 2, wcopy[i])
            if 1 <= k <= FINE:
                if k - 1 >= SINGLE:
                    y_store(k - 1, 0, 4, 1)
                elif units[k - 1][1] % 2 == 1:
                    y_store(k - 1, 0, 4, 2)
            if k >= 1 and casts[3] == "v":
                y_round(k - 1, 3, "v")
            if side:
                h_quantize(n)
            if k >= 2:
                y_quantize(k - 2, 0, 4)
                if units[k - 2][1] == G - 1:
                    scale_store(units[k - 2][0])
        for j0, j1 in LAST_GROUPS:
            y_transpose(last, j0, j1)
            y_copy(last, j0, j1, "a")
            y_quantize(last, j0, j1)
        scale_store(len(CHUNKS) - 1)
